import numpy as np
import ml_dtypes


def mxq(x, axis, fmt="e4m3"):
    dtype, down = {"e4m3": (ml_dtypes.float8_e4m3fn, 7), "e5m2": (ml_dtypes.float8_e5m2, 14)}[fmt]
    v = np.moveaxis(np.asarray(x, np.float32).astype(ml_dtypes.bfloat16).astype(np.float64), axis, -1)
    blocks = v.reshape(v.shape[:-1] + (-1, 32))
    amax = np.abs(blocks).max(-1, keepdims=True)
    byte = np.maximum(np.where(amax > 0, np.frexp(amax)[1] - 1 + 127, 0) - down, 1)
    scale = np.exp2(byte - 127.0)
    codes = (blocks / scale).astype(np.float32).astype(dtype).astype(np.float64)
    return np.moveaxis((codes * scale).reshape(v.shape), -1, axis)


WIDE = False


def mx_kscale(k):
    if not WIDE:
        return np.ones(k)
    levels = np.array([24, -24, 12, -12, 0])
    if k % 512:
        return np.exp2(np.random.permutation(np.resize(levels, k // 32))).repeat(32)
    a = np.empty((k // 512, 16))
    for p in range(k // 512):
        a[p, :8] = np.random.permutation(np.resize(levels, 8))
        for g in range(8):
            far = levels[np.abs(levels - a[p, g]) >= 10]
            a[p, g + 8] = far[np.random.randint(len(far))]
    return np.exp2(a.ravel()).repeat(32)


def f64(x):
    return np.asarray(x).astype(np.float64)


def striped8(idx):
    return np.concatenate([v.reshape(-1, 16).T for v in idx]).astype(np.uint16)


def unstriped8(offs):
    return np.stack([offs[16 * g:16 * g + 16].T.reshape(-1) for g in range(8)]).astype(np.int64)


E2M1 = np.array([0.0, 0.5, 1.0, 1.5, 2.0, 3.0, 4.0, 6.0, -0.0, -0.5, -1.0, -1.5, -2.0, -3.0, -4.0, -6.0])


def pack_weight(w, fmt):
    k, n = w.shape
    w = f64(np.asarray(w, np.float32).astype(ml_dtypes.bfloat16)).reshape(k // 32, 32, n)
    amax = np.abs(w).max(1)
    if fmt == "e4m3":
        byte = np.frexp(amax)[1] - 1 + 127 - 7
    else:
        mant, ex = np.frexp(amax / 6.0)
        byte = np.where(mant > 0.5, ex, ex - 1) + 127
    byte = np.clip(np.where(amax > 0, byte, 1), 1, 254)
    scaled = (w * np.exp2(127.0 - byte)[:, None, :]).reshape(k, n).astype(np.float32)
    by_word = np.ascontiguousarray(scaled.reshape(k // 512, 128, 4, n).transpose(0, 1, 3, 2))
    if fmt == "e4m3":
        words = by_word.astype(ml_dtypes.float8_e4m3fn).view(np.uint8)
    else:
        c = by_word.astype(ml_dtypes.float4_e2m1fn).view(np.uint8) & 0xF
        words = (c[..., 0::2] | (c[..., 1::2] << 4)).reshape(k // 512, 128, 2 * n)
    return np.ascontiguousarray(words), np.ascontiguousarray(byte.astype(np.uint8).reshape(k // 512, 16, n))


def unpack_weight(words, scales, fmt):
    g, _, n = scales.shape
    words = np.ascontiguousarray(words).reshape(g, 128, n, -1)
    if fmt == "e4m3":
        vals = words.view(ml_dtypes.float8_e4m3fn).astype(np.float64)
    else:
        nib = np.empty((g, 128, n, 4), np.uint8)
        nib[..., 0::2] = words & 0xF
        nib[..., 1::2] = words >> 4
        vals = E2M1[nib]
    vals = vals * np.repeat(np.exp2(scales.astype(np.float64) - 127.0), 8, axis=1)[..., None]
    return vals.transpose(0, 1, 3, 2).reshape(g * 512, n)


def planes(y):
    n, m = y.shape
    v = y.astype(np.float32).astype(ml_dtypes.bfloat16).astype(np.float64).reshape(n // 32, 32, m)
    top = np.abs(v).max(1)
    byte = np.clip(np.where(top > 0, np.frexp(top)[1] - 1 + 127 - 7, 1), 1, 254)
    codes = (v * np.exp2(127.0 - byte)[:, None, :]).reshape(n, m).astype(np.float32).astype(ml_dtypes.float8_e4m3fn).view(np.uint8)
    words = codes.reshape(n // 512, 128, 4, m).transpose(0, 1, 3, 2)
    return np.ascontiguousarray(words), np.ascontiguousarray(byte.astype(np.uint8).reshape(n // 512, 16, m))


def sigm(f):
    return 1.0 / (1.0 + np.exp(-np.maximum(f, -700.0)))


K, N, T, J = 512, 512, 2048, 1024


def setup_inputs():
    n = np.random.standard_normal
    s = mx_kscale(K)[:, None]
    p_wk = pack_weight(n((K, N)) / np.sqrt(K) / s, "e4m3")
    p_wv = pack_weight(n((K, N)) / np.sqrt(K) / s, "e4m3")
    return {
        "xT": (n((K, T)) * s).astype(np.float32),
        "wgt": np.repeat(np.random.uniform(0.5, 2.0, (8, J)), 16, axis=0).astype(np.float32),
        "wk_words": p_wk[0],
        "wk_scales": p_wk[1],
        "wv_words": p_wv[0],
        "wv_scales": p_wv[1],
        "bg": (0.3 * n(N) - 1.0).astype(np.float32),
        "res": (n((N, J))).astype(np.float32),
        "offs": striped8(np.stack([np.random.permutation(T)[:J] for _ in range(8)])),
    }


def reference(xT, wgt, wk_words, wk_scales, wv_words, wv_scales, bg, res, offs):
    idx = unstriped8(offs)
    rows = np.arange(K)
    xg = f64(wgt)[rows // 4 % 128] * f64(xT)[rows[:, None], idx[rows % 512 // 64]]
    xT_ = mxq(xg, 0, "e4m3")
    wk_ = unpack_weight(wk_words, wk_scales, "e4m3")
    wv_ = unpack_weight(wv_words, wv_scales, "e4m3")
    ke = wk_.T @ xT_
    ve = wv_.T @ xT_
    gate = sigm(ke + f64(bg)[:, None])
    out_0 = f64(res) + gate * (ve - f64(res))
    return (out_0,) + planes(out_0)

@@ -1,0 +1,212 @@
+from contextlib import ExitStack
+
+import concourse.mybir as mybir
+
+K, N, T, J = 512, 512, 2048, 1024
+FLOPS = 2 * 2 * K * N * J
+
+F32 = mybir.dt.float32
+BF16 = mybir.dt.bfloat16
+I32 = mybir.dt.int32
+U32 = mybir.dt.uint32
+U16 = mybir.dt.uint16
+U8 = mybir.dt.uint8
+FP8X4 = mybir.dt.float8_e4m3fn_x4
+MULT = mybir.AluOpType.mult
+ADD = mybir.AluOpType.add
+SUB = mybir.AluOpType.subtract
+SIGMOID = mybir.ActivationFunctionType.Sigmoid
+
+P = 128
+PACK = 4
+BANK = 512
+LIST_ROWS = 16
+WIDTHS = [256, 256, 256, 128, 128]
+WV_ROW = 4
+
+
+def tile_list_hwayP_kernel(
+    tc, xT, wgt, wk_words, wk_scales, wv_words, wv_scales, bg, res, offs, out_0, out_1, out_2
+):
+    nc = tc.nc
+    chunks = range(len(WIDTHS))
+    starts = [sum(WIDTHS[:c]) for c in chunks]
+    cols = [slice(starts[c], starts[c] + WIDTHS[c]) for c in chunks]
+
+    with ExitStack() as ctx:
+        keep = ctx.enter_context(tc.tile_pool(name="keep", bufs=1))
+        psum = ctx.enter_context(tc.psum_pool(name="psum", bufs=2))
+
+        def tiles(name, shape_of, dtype):
+            return [keep.tile(shape_of(WIDTHS[c]), dtype, name=f"{name}{c}", align_bytes=64) for c in chunks]
+
+        offsets = keep.tile([P, J // LIST_ROWS], U16, name="offsets")
+        nc.sync.dma_start(offsets[:], offs)
+        ws_raw = keep.tile([P, N], U8, name="ws_raw")
+        nc.vector.memset(ws_raw[:].bitcast(I32), 0)
+        for q in range(4):
+            nc.gpsimd.dma_start(
+                ws_raw[32 * q : 32 * q + 4, :].bitcast(I32), wk_scales[0, 4 * q : 4 * q + 4, :].bitcast(I32)
+            )
+            nc.scalar.dma_start(
+                ws_raw[32 * q + WV_ROW : 32 * q + WV_ROW + 4, :].bitcast(I32),
+                wv_scales[0, 4 * q : 4 * q + 4, :].bitcast(I32),
+            )
+        bg_sb = keep.tile([P, PACK], F32, name="bg_sb")
+        nc.scalar.dma_start(bg_sb[:], bg.rearrange("(p t) -> p t", t=PACK))
+
+        wgt_sb = keep.tile([P, J], F32, name="wgt_sb")
+        nc.sync.dma_start(wgt_sb[:], wgt)
+        x_rows = xT.rearrange("(p t) s -> p t s", t=PACK)
+        x_sb = [keep.tile([P, T], F32, name=f"x{t}", align_bytes=64) for t in range(PACK)]
+        for t in range(PACK):
+            nc.sync.dma_start(x_sb[t][:], x_rows[:, t, :])
+        wk_raw = keep.tile([P, N], I32, name="wk_raw")
+        wv_raw = keep.tile([P, N], I32, name="wv_raw")
+        nc.sync.dma_start(wk_raw[:], wk_words[0].rearrange("p n i -> p (n i)").bitcast(I32))
+        nc.sync.dma_start(wv_raw[:], wv_words[0].rearrange("p n i -> p (n i)").bitcast(I32))
+        res_rows = res.rearrange("(p t) j -> p t j", t=PACK)
+        res_sb = tiles("res", lambda w: [P, PACK, w], F32)
+        for c in chunks:
+            nc.sync.dma_start(res_sb[c][:], res_rows[:, :, cols[c]])
+
+        warm_in = keep.tile([P, 1], F32, name="warm_in")
+        warm_out = keep.tile([P, 1], F32, name="warm_out")
+        nc.vector.memset(warm_in[:], 0.0)
+        nc.scalar.activation(warm_out[:], warm_in[:], SIGMOID)
+
+        picked = [keep.tile([P, 2, J], F32, name=f"picked{u}") for u in range(2)]
+        xg_bf = tiles("xg_bf", lambda w: [P, w, PACK], BF16)
+        xg_codes = tiles("xg_codes", lambda w: [P, w], U32)
+        xg_scales = tiles("xg_scales", lambda w: [P, w], U8)
+        wk_codes = keep.tile([P, N], I32, name="wk_codes", align_bytes=64)
+        wv_codes = keep.tile([P, N], I32, name="wv_codes", align_bytes=64)
+        gate = tiles("gate", lambda w: [P, PACK, w], F32)
+        diff = tiles("diff", lambda w: [P, PACK, w], F32)
+        step = tiles("step", lambda w: [P, PACK, w], F32)
+        y = tiles("y", lambda w: [P, PACK, w], F32)
+        y_bf = tiles("y_bf", lambda w: [P, w, PACK], BF16)
+        y_codes = tiles("y_codes", lambda w: [P, w], U32)
+        y_scales = keep.tile([P, J], U8, name="y_scales", align_bytes=64)
+        out_rows = out_0.rearrange("(p t) j -> p t j", t=PACK)
+        out_words = out_1[0].rearrange("p j i -> p (j i)").bitcast(I32)
+
+        def gather(t, js):
+            entries = offsets[:, js.start // LIST_ROWS : js.stop // LIST_ROWS]
+            nc.vector.tensor_tensor(picked[t // 2][:, t % 2, js], x_sb[t][:].indirect(entries), wgt_sb[:, js], MULT)
+
+        def round_pair(u, c):
+            nc.scalar.copy(
+                xg_bf[c][:, :, 2 * u : 2 * u + 2].rearrange("p (b i) e -> p b e i", i=4),
+                picked[u][:, :, cols[c]].rearrange("p e (b i) -> p b e i", i=4),
+            )
+
+        def quantize_xg(c):
+            nc.vector.quantize_mx(
+                out=xg_codes[c][:].bitcast(FP8X4),
+                scales=xg_scales[c][:],
+                in_=xg_bf[c][:].rearrange("p j t -> p (j t)"),
+            )
+
+        def deal_words(codes, raw):
+            nc.vector.tensor_copy(
+                codes[:].rearrange("p (t b i) -> p b t i", t=PACK, i=4),
+                raw[:].rearrange("p (b i t) -> p b t i", t=PACK, i=4),
+            )
+
+        def groups(c):
+            per_bank = BANK // WIDTHS[c]
+            return [slice(t0, t0 + per_bank) for t0 in range(0, PACK, per_bank)]
+
+        ve_banks = {}
+
+        def multiply(c):
+            for g, ts in enumerate(groups(c)):
+                shape = [P, ts.stop - ts.start, WIDTHS[c]]
+                ke = psum.tile(shape, F32, name=f"ke{g}")
+                ve = psum.tile(shape, F32, name=f"ve{g}")
+                for bank, codes, row in ((ke, wk_codes, 0), (ve, wv_codes, WV_ROW)):
+                    for t in range(ts.start, ts.stop):
+                        ms = slice(P * t, P * (t + 1))
+                        nc.tensor.matmul_mx(
+                            out=bank[:, t - ts.start, :],
+                            lhsT=codes[:, ms].bitcast(FP8X4),
+                            lhsT_scale=w_scales[row:P, ms],
+                            rhs=xg_codes[c][:].bitcast(FP8X4),
+                            rhs_scale=xg_scales[c][:],
+                            start=True,
+                            stop=True,
+                        )
+                for t in range(ts.start, ts.stop):
+                    nc.scalar.activation(
+                        gate[c][:, t, :], ke[:, t - ts.start, :], SIGMOID, bias=bg_sb[:, t : t + 1]
+                    )
+                ve_banks[c, g] = ve
+
+        def subtract(c):
+            for g, ts in enumerate(groups(c)):
+                nc.vector.tensor_tensor(diff[c][:, ts, :], ve_banks[c, g][:], res_sb[c][:, ts, :], SUB)
+
+        def apply_gate(c):
+            for ts in groups(c):
+                nc.vector.tensor_tensor(step[c][:, ts, :], diff[c][:, ts, :], gate[c][:, ts, :], MULT)
+
+        def finish(c):
+            for ts in groups(c):
+                nc.vector.tensor_tensor(y[c][:, ts, :], step[c][:, ts, :], res_sb[c][:, ts, :], ADD)
+            nc.sync.dma_start(out_rows[:, :, cols[c]], y[c][:])
+            nc.scalar.copy(
+                y_bf[c][:].rearrange("p (b i) t -> p b t i", i=4),
+                y[c][:].rearrange("p t (b i) -> p b t i", i=4),
+            )
+
+        def quantize_y(c):
+            nc.vector.quantize_mx(
+                out=y_codes[c][:].bitcast(FP8X4),
+                scales=y_scales[:, cols[c]],
+                in_=y_bf[c][:].rearrange("p j t -> p (j t)"),
+            )
+            nc.sync.dma_start(out_words[:, cols[c]], y_codes[c][:].bitcast(I32))
+
+        whole = slice(0, J)
+        gather(0, whole)
+        gather(1, whole)
+        for c in chunks:
+            round_pair(0, c)
+        w_scales = keep.tile([P, N], U8, name="w_scales", tag="x1", align_bytes=64)
+        nc.vector.tensor_copy(
+            w_scales[:].rearrange("p (t m) -> p t m", t=PACK), ws_raw[:].rearrange("p (m t) -> p t m", t=PACK)
+        )
+        gather(2, whole)
+
+        last = len(WIDTHS) - 1
+        gather(3, cols[0])
+        round_pair(1, 0)
+        gather(3, cols[1])
+        round_pair(1, 1)
+        deal_words(wk_codes, wk_raw)
+        deal_words(wv_codes, wv_raw)
+        quantize_xg(0)
+        multiply(0)
+        for c in range(2, last + 1):
+            gather(3, cols[c])
+            round_pair(1, c)
+        quantize_xg(1)
+        for c in chunks:
+            if c + 1 <= last:
+                multiply(c + 1)
+            subtract(c)
+            if c >= 1:
+                finish(c - 1)
+            apply_gate(c)
+            if c + 2 <= last:
+                quantize_xg(c + 2)
+            if c >= 1:
+                quantize_y(c - 1)
+        finish(last)
+        quantize_y(last)
+
+        out_scale_rows = out_2[0].bitcast(I32)
+        for q in range(4):
+            queue = nc.sync if q % 2 == 0 else nc.scalar
+            queue.dma_start(out_scale_rows[4 * q : 4 * q + 4, :], y_scales[32 * q : 32 * q + 4, :].bitcast(I32))

@@ -21,7 +21,7 @@ P = 128
 PACK = 4
 BANK = 512
 LIST_ROWS = 16
-WIDTHS = [256, 256, 256, 128, 128]
+WIDTHS = [128, 256, 256, 256, 128]
 WV_ROW = 4
 
 
@@ -44,27 +44,30 @@ def tile_list_hwayP_kernel(
         nc.sync.dma_start(offsets[:], offs)
         ws_raw = keep.tile([P, N], U8, name="ws_raw")
         nc.vector.memset(ws_raw[:].bitcast(I32), 0)
-        for q in range(4):
-            nc.gpsimd.dma_start(
-                ws_raw[32 * q : 32 * q + 4, :].bitcast(I32), wk_scales[0, 4 * q : 4 * q + 4, :].bitcast(I32)
-            )
-            nc.scalar.dma_start(
-                ws_raw[32 * q + WV_ROW : 32 * q + WV_ROW + 4, :].bitcast(I32),
-                wv_scales[0, 4 * q : 4 * q + 4, :].bitcast(I32),
-            )
-        bg_sb = keep.tile([P, PACK], F32, name="bg_sb")
-        nc.scalar.dma_start(bg_sb[:], bg.rearrange("(p t) -> p t", t=PACK))
+
+        def load_scales(scales, row):
+            for q in range(4):
+                nc.sync.dma_start(
+                    ws_raw[32 * q + row : 32 * q + row + 4, :].bitcast(I32),
+                    scales[0, 4 * q : 4 * q + 4, :].bitcast(I32),
+                )
 
         wgt_sb = keep.tile([P, J], F32, name="wgt_sb")
         nc.sync.dma_start(wgt_sb[:], wgt)
         x_rows = xT.rearrange("(p t) s -> p t s", t=PACK)
         x_sb = [keep.tile([P, T], F32, name=f"x{t}", align_bytes=64) for t in range(PACK)]
-        for t in range(PACK):
+        for t in (0, 1):
             nc.sync.dma_start(x_sb[t][:], x_rows[:, t, :])
+        load_scales(wk_scales, 0)
+        nc.sync.dma_start(x_sb[2][:], x_rows[:, 2, :])
+        load_scales(wv_scales, WV_ROW)
         wk_raw = keep.tile([P, N], I32, name="wk_raw")
         wv_raw = keep.tile([P, N], I32, name="wv_raw")
         nc.sync.dma_start(wk_raw[:], wk_words[0].rearrange("p n i -> p (n i)").bitcast(I32))
         nc.sync.dma_start(wv_raw[:], wv_words[0].rearrange("p n i -> p (n i)").bitcast(I32))
+        nc.sync.dma_start(x_sb[3][:], x_rows[:, 3, :])
+        bg_sb = keep.tile([P, PACK], F32, name="bg_sb")
+        nc.sync.dma_start(bg_sb[:], bg.rearrange("(p t) -> p t", t=PACK))
         res_rows = res.rearrange("(p t) j -> p t j", t=PACK)
         res_sb = tiles("res", lambda w: [P, PACK, w], F32)
         for c in chunks:
@@ -125,7 +128,7 @@ def tile_list_hwayP_kernel(
                 shape = [P, ts.stop - ts.start, WIDTHS[c]]
                 ke = psum.tile(shape, F32, name=f"ke{g}")
                 ve = psum.tile(shape, F32, name=f"ve{g}")
-                for bank, codes, row in ((ke, wk_codes, 0), (ve, wv_codes, WV_ROW)):
+                for bank, codes, row in ((ve, wv_codes, WV_ROW), (ke, wk_codes, 0)):
                     for t in range(ts.start, ts.stop):
                         ms = slice(P * t, P * (t + 1))
                         nc.tensor.matmul_mx(
@@ -152,8 +155,10 @@ def tile_list_hwayP_kernel(
                 nc.vector.tensor_tensor(step[c][:, ts, :], diff[c][:, ts, :], gate[c][:, ts, :], MULT)
 
         def finish(c):
-            for ts in groups(c):
-                nc.vector.tensor_tensor(y[c][:, ts, :], step[c][:, ts, :], res_sb[c][:, ts, :], ADD)
+            shared = PACK * WIDTHS[c + 1] // (2 * WIDTHS[c]) if c < last else 0
+            for engine, ts in ((nc.gpsimd, slice(0, shared)), (nc.vector, slice(shared, PACK))):
+                if ts.stop > ts.start:
+                    engine.tensor_tensor(y[c][:, ts, :], step[c][:, ts, :], res_sb[c][:, ts, :], ADD)
             nc.sync.dma_start(out_rows[:, :, cols[c]], y[c][:])
             nc.scalar.copy(
                 y_bf[c][:].rearrange("p (b i) t -> p b t i", i=4),
@@ -173,37 +178,37 @@ def tile_list_hwayP_kernel(
         gather(1, whole)
         for c in chunks:
             round_pair(0, c)
-        w_scales = keep.tile([P, N], U8, name="w_scales", tag="x1", align_bytes=64)
+        gather(2, whole)
+        w_scales = keep.tile([P, N], U8, name="w_scales", align_bytes=64)
         nc.vector.tensor_copy(
             w_scales[:].rearrange("p (t m) -> p t m", t=PACK), ws_raw[:].rearrange("p (m t) -> p t m", t=PACK)
         )
-        gather(2, whole)
+        deal_words(wk_codes, wk_raw)
+        deal_words(wv_codes, wv_raw)
 
         last = len(WIDTHS) - 1
         gather(3, cols[0])
         round_pair(1, 0)
         gather(3, cols[1])
         round_pair(1, 1)
-        deal_words(wk_codes, wk_raw)
-        deal_words(wv_codes, wv_raw)
         quantize_xg(0)
         multiply(0)
         for c in range(2, last + 1):
             gather(3, cols[c])
             round_pair(1, c)
         quantize_xg(1)
+        multiply(1)
+        subtract(0)
         for c in chunks:
-            if c + 1 <= last:
-                multiply(c + 1)
-            subtract(c)
-            if c >= 1:
-                finish(c - 1)
-            apply_gate(c)
             if c + 2 <= last:
                 quantize_xg(c + 2)
+                multiply(c + 2)
+            apply_gate(c)
+            if c + 1 <= last:
+                subtract(c + 1)
+            finish(c)
             if c >= 1:
                 quantize_y(c - 1)
-        finish(last)
         quantize_y(last)
 
         out_scale_rows = out_2[0].bitcast(I32)

@@ -155,10 +155,7 @@ def tile_list_hwayP_kernel(
                 nc.vector.tensor_tensor(step[c][:, ts, :], diff[c][:, ts, :], gate[c][:, ts, :], MULT)
 
         def finish(c):
-            shared = PACK * WIDTHS[c + 1] // (2 * WIDTHS[c]) if c < last else 0
-            for engine, ts in ((nc.gpsimd, slice(0, shared)), (nc.vector, slice(shared, PACK))):
-                if ts.stop > ts.start:
-                    engine.tensor_tensor(y[c][:, ts, :], step[c][:, ts, :], res_sb[c][:, ts, :], ADD)
+            nc.vector.tensor_tensor(y[c][:], step[c][:], res_sb[c][:], ADD)
             nc.sync.dma_start(out_rows[:, :, cols[c]], y[c][:])
             nc.scalar.copy(
                 y_bf[c][:].rearrange("p (b i) t -> p b t i", i=4),

from contextlib import ExitStack

import concourse.mybir as mybir

K, N, T, J = 512, 512, 2048, 1024
FLOPS = 2 * 2 * K * N * J

F32 = mybir.dt.float32
BF16 = mybir.dt.bfloat16
I32 = mybir.dt.int32
U32 = mybir.dt.uint32
U16 = mybir.dt.uint16
U8 = mybir.dt.uint8
FP8X4 = mybir.dt.float8_e4m3fn_x4
MULT = mybir.AluOpType.mult
ADD = mybir.AluOpType.add
SUB = mybir.AluOpType.subtract
SIGMOID = mybir.ActivationFunctionType.Sigmoid

P = 128
PACK = 4
BANK = 512
LIST_ROWS = 16
WIDTHS = [128, 256, 256, 256, 128]
WV_ROW = 4


def tile_list_hwayP_kernel(
    tc, xT, wgt, wk_words, wk_scales, wv_words, wv_scales, bg, res, offs, out_0, out_1, out_2
):
    nc = tc.nc
    chunks = range(len(WIDTHS))
    starts = [sum(WIDTHS[:c]) for c in chunks]
    cols = [slice(starts[c], starts[c] + WIDTHS[c]) for c in chunks]

    with ExitStack() as ctx:
        keep = ctx.enter_context(tc.tile_pool(name="keep", bufs=1))
        psum = ctx.enter_context(tc.psum_pool(name="psum", bufs=2))

        def tiles(name, shape_of, dtype):
            return [keep.tile(shape_of(WIDTHS[c]), dtype, name=f"{name}{c}", align_bytes=64) for c in chunks]

        offsets = keep.tile([P, J // LIST_ROWS], U16, name="offsets")
        nc.sync.dma_start(offsets[:], offs)
        ws_raw = keep.tile([P, N], U8, name="ws_raw")
        nc.vector.memset(ws_raw[:].bitcast(I32), 0)

        def load_scales(scales, row):
            for q in range(4):
                nc.sync.dma_start(
                    ws_raw[32 * q + row : 32 * q + row + 4, :].bitcast(I32),
                    scales[0, 4 * q : 4 * q + 4, :].bitcast(I32),
                )

        wgt_sb = keep.tile([P, J], F32, name="wgt_sb")
        nc.sync.dma_start(wgt_sb[:], wgt)
        x_rows = xT.rearrange("(p t) s -> p t s", t=PACK)
        x_sb = [keep.tile([P, T], F32, name=f"x{t}", align_bytes=64) for t in range(PACK)]
        for t in (0, 1):
            nc.sync.dma_start(x_sb[t][:], x_rows[:, t, :])
        load_scales(wk_scales, 0)
        nc.sync.dma_start(x_sb[2][:], x_rows[:, 2, :])
        load_scales(wv_scales, WV_ROW)
        wk_raw = keep.tile([P, N], I32, name="wk_raw")
        wv_raw = keep.tile([P, N], I32, name="wv_raw")
        nc.sync.dma_start(wk_raw[:], wk_words[0].rearrange("p n i -> p (n i)").bitcast(I32))
        nc.sync.dma_start(wv_raw[:], wv_words[0].rearrange("p n i -> p (n i)").bitcast(I32))
        nc.sync.dma_start(x_sb[3][:], x_rows[:, 3, :])
        bg_sb = keep.tile([P, PACK], F32, name="bg_sb")
        nc.sync.dma_start(bg_sb[:], bg.rearrange("(p t) -> p t", t=PACK))
        res_rows = res.rearrange("(p t) j -> p t j", t=PACK)
        res_sb = tiles("res", lambda w: [P, PACK, w], F32)
        for c in chunks:
            nc.sync.dma_start(res_sb[c][:], res_rows[:, :, cols[c]])

        warm_in = keep.tile([P, 1], F32, name="warm_in")
        warm_out = keep.tile([P, 1], F32, name="warm_out")
        nc.vector.memset(warm_in[:], 0.0)
        nc.scalar.activation(warm_out[:], warm_in[:], SIGMOID)

        picked = [keep.tile([P, 2, J], F32, name=f"picked{u}") for u in range(2)]
        xg_bf = tiles("xg_bf", lambda w: [P, w, PACK], BF16)
        xg_codes = tiles("xg_codes", lambda w: [P, w], U32)
        xg_scales = tiles("xg_scales", lambda w: [P, w], U8)
        wk_codes = keep.tile([P, N], I32, name="wk_codes", align_bytes=64)
        wv_codes = keep.tile([P, N], I32, name="wv_codes", align_bytes=64)
        gate = tiles("gate", lambda w: [P, PACK, w], F32)
        diff = tiles("diff", lambda w: [P, PACK, w], F32)
        step = tiles("step", lambda w: [P, PACK, w], F32)
        y = tiles("y", lambda w: [P, PACK, w], F32)
        y_bf = tiles("y_bf", lambda w: [P, w, PACK], BF16)
        y_codes = tiles("y_codes", lambda w: [P, w], U32)
        y_scales = keep.tile([P, J], U8, name="y_scales", align_bytes=64)
        out_rows = out_0.rearrange("(p t) j -> p t j", t=PACK)
        out_words = out_1[0].rearrange("p j i -> p (j i)").bitcast(I32)

        def gather(t, js):
            entries = offsets[:, js.start // LIST_ROWS : js.stop // LIST_ROWS]
            nc.vector.tensor_tensor(picked[t // 2][:, t % 2, js], x_sb[t][:].indirect(entries), wgt_sb[:, js], MULT)

        def round_pair(u, c):
            nc.scalar.copy(
                xg_bf[c][:, :, 2 * u : 2 * u + 2].rearrange("p (b i) e -> p b e i", i=4),
                picked[u][:, :, cols[c]].rearrange("p e (b i) -> p b e i", i=4),
            )

        def quantize_xg(c):
            nc.vector.quantize_mx(
                out=xg_codes[c][:].bitcast(FP8X4),
                scales=xg_scales[c][:],
                in_=xg_bf[c][:].rearrange("p j t -> p (j t)"),
            )

        def deal_words(codes, raw):
            nc.vector.tensor_copy(
                codes[:].rearrange("p (t b i) -> p b t i", t=PACK, i=4),
                raw[:].rearrange("p (b i t) -> p b t i", t=PACK, i=4),
            )

        def groups(c):
            per_bank = BANK // WIDTHS[c]
            return [slice(t0, t0 + per_bank) for t0 in range(0, PACK, per_bank)]

        ve_banks = {}

        def multiply(c):
            for g, ts in enumerate(groups(c)):
                shape = [P, ts.stop - ts.start, WIDTHS[c]]
                ke = psum.tile(shape, F32, name=f"ke{g}")
                ve = psum.tile(shape, F32, name=f"ve{g}")
                for bank, codes, row in ((ve, wv_codes, WV_ROW), (ke, wk_codes, 0)):
                    for t in range(ts.start, ts.stop):
                        ms = slice(P * t, P * (t + 1))
                        nc.tensor.matmul_mx(
                            out=bank[:, t - ts.start, :],
                            lhsT=codes[:, ms].bitcast(FP8X4),
                            lhsT_scale=w_scales[row:P, ms],
                            rhs=xg_codes[c][:].bitcast(FP8X4),
                            rhs_scale=xg_scales[c][:],
                            start=True,
                            stop=True,
                        )
                for t in range(ts.start, ts.stop):
                    nc.scalar.activation(
                        gate[c][:, t, :], ke[:, t - ts.start, :], SIGMOID, bias=bg_sb[:, t : t + 1]
                    )
                ve_banks[c, g] = ve

        def subtract(c):
            for g, ts in enumerate(groups(c)):
                nc.vector.tensor_tensor(diff[c][:, ts, :], ve_banks[c, g][:], res_sb[c][:, ts, :], SUB)

        def apply_gate(c):
            for ts in groups(c):
                nc.vector.tensor_tensor(step[c][:, ts, :], diff[c][:, ts, :], gate[c][:, ts, :], MULT)

        def finish(c):
            nc.vector.tensor_tensor(y[c][:], step[c][:], res_sb[c][:], ADD)
            nc.sync.dma_start(out_rows[:, :, cols[c]], y[c][:])
            nc.scalar.copy(
                y_bf[c][:].rearrange("p (b i) t -> p b t i", i=4),
                y[c][:].rearrange("p t (b i) -> p b t i", i=4),
            )

        def quantize_y(c):
            nc.vector.quantize_mx(
                out=y_codes[c][:].bitcast(FP8X4),
                scales=y_scales[:, cols[c]],
                in_=y_bf[c][:].rearrange("p j t -> p (j t)"),
            )
            nc.sync.dma_start(out_words[:, cols[c]], y_codes[c][:].bitcast(I32))

        whole = slice(0, J)
        gather(0, whole)
        gather(1, whole)
        for c in chunks:
            round_pair(0, c)
        gather(2, whole)
        w_scales = keep.tile([P, N], U8, name="w_scales", align_bytes=64)
        nc.vector.tensor_copy(
            w_scales[:].rearrange("p (t m) -> p t m", t=PACK), ws_raw[:].rearrange("p (m t) -> p t m", t=PACK)
        )
        deal_words(wk_codes, wk_raw)
        deal_words(wv_codes, wv_raw)

        last = len(WIDTHS) - 1
        gather(3, cols[0])
        round_pair(1, 0)
        gather(3, cols[1])
        round_pair(1, 1)
        quantize_xg(0)
        multiply(0)
        for c in range(2, last + 1):
            gather(3, cols[c])
            round_pair(1, c)
        quantize_xg(1)
        multiply(1)
        subtract(0)
        for c in chunks:
            if c + 2 <= last:
                quantize_xg(c + 2)
                multiply(c + 2)
            apply_gate(c)
            if c + 1 <= last:
                subtract(c + 1)
            finish(c)
            if c >= 1:
                quantize_y(c - 1)
        quantize_y(last)

        out_scale_rows = out_2[0].bitcast(I32)
        for q in range(4):
            queue = nc.sync if q % 2 == 0 else nc.scalar
            queue.dma_start(out_scale_rows[4 * q : 4 * q + 4, :], y_scales[32 * q : 32 * q + 4, :].bitcast(I32))
